import numpy as np
import ml_dtypes


def mxq(x, axis, fmt="e4m3"):
    dtype, down = {"e4m3": (ml_dtypes.float8_e4m3fn, 7), "e5m2": (ml_dtypes.float8_e5m2, 14)}[fmt]
    v = np.moveaxis(np.asarray(x, np.float32).astype(ml_dtypes.bfloat16).astype(np.float64), axis, -1)
    blocks = v.reshape(v.shape[:-1] + (-1, 32))
    amax = np.abs(blocks).max(-1, keepdims=True)
    byte = np.maximum(np.where(amax > 0, np.frexp(amax)[1] - 1 + 127, 0) - down, 1)
    scale = np.exp2(byte - 127.0)
    codes = (blocks / scale).astype(np.float32).astype(dtype).astype(np.float64)
    return np.moveaxis((codes * scale).reshape(v.shape), -1, axis)


WIDE = False


def mx_kscale(k):
    if not WIDE:
        return np.ones(k)
    levels = np.array([10, -10, 5, -5, 0])
    if k % 512:
        return np.exp2(np.random.permutation(np.resize(levels, k // 32))).repeat(32)
    a = np.empty((k // 512, 16))
    for p in range(k // 512):
        a[p, :8] = np.random.permutation(np.resize(levels, 8))
        for g in range(8):
            far = levels[np.abs(levels - a[p, g]) >= 10]
            a[p, g + 8] = far[np.random.randint(len(far))]
    return np.exp2(a.ravel()).repeat(32)


def f64(x):
    return np.asarray(x).astype(np.float64)


def striped(idx):
    return np.tile(idx.reshape(-1, 16).T, (8, 1)).astype(np.uint16)


def unstriped(offs):
    return offs[:16].T.reshape(-1).astype(np.int64)


def striped8(idx):
    return np.concatenate([x.reshape(-1, 16).T for x in idx]).astype(np.uint16)


def runs(offs, k):
    lists = np.stack([offs[16 * r : 16 * r + 16].T.reshape(-1) for r in range(8)]).astype(np.int64)
    return lists[np.arange(k) % 512 // 64]


def pack_weight(w):
    k, n = w.shape
    w = f64(np.asarray(w, np.float32).astype(ml_dtypes.bfloat16)).reshape(k // 32, 32, n)
    amax = np.abs(w).max(1)
    byte = np.clip(np.where(amax > 0, np.frexp(amax)[1] - 1 + 127 - 7, 1), 1, 254)
    scaled = (w * np.exp2(127.0 - byte)[:, None, :]).reshape(k, n).astype(np.float32)
    words = np.ascontiguousarray(scaled.reshape(k // 512, 128, 4, n).transpose(0, 1, 3, 2)).astype(ml_dtypes.float8_e4m3fn).view(np.uint8)
    return words, np.ascontiguousarray(byte.astype(np.uint8).reshape(k // 512, 16, n))


def unpack_weight(words, scales):
    g, p, n, _ = words.shape
    vals = np.ascontiguousarray(words).view(ml_dtypes.float8_e4m3fn).astype(np.float64) * np.repeat(np.exp2(scales.astype(np.float64) - 127.0), 8, axis=1)[..., None]
    return vals.transpose(0, 1, 3, 2).reshape(g * 512, n)

def planes(y):
    n, m = y.shape
    v = y.astype(np.float32).astype(ml_dtypes.bfloat16).astype(np.float64).reshape(n // 32, 32, m)
    top = np.abs(v).max(1)
    byte = np.clip(np.where(top > 0, np.frexp(top)[1] - 1 + 127 - 7, 1), 1, 254)
    codes = (v * np.exp2(127.0 - byte)[:, None, :]).reshape(n, m).astype(np.float32).astype(ml_dtypes.float8_e4m3fn).view(np.uint8)
    words = codes.reshape(n // 512, 128, 4, m).transpose(0, 1, 3, 2)
    return np.ascontiguousarray(words), np.ascontiguousarray(byte.astype(np.uint8).reshape(n // 512, 16, m))


K, T, S, G, H, W = 512, 1024, 256, 2048, 512, 128


def setup_inputs():
    n = np.random.standard_normal
    s = mx_kscale(K)[:, None]
    packed_xT = pack_weight(n((K, T)) * s)
    packed_dT = pack_weight(n((K, G)) / s)
    perm = np.random.permutation(S)
    perm2 = np.random.permutation(S)
    perm3 = np.random.permutation(S)
    return {
        "x_words": packed_xT[0],
        "x_scales": packed_xT[1],
        "d_words": packed_dT[0],
        "d_scales": packed_dT[1],
        "gs": (np.random.uniform(0.5, 1.5, (K, 1)) * s).astype(np.float32),
        "offs": striped(np.random.permutation(T)[:S]),
        "k1": striped8(np.random.randint(0, G, (8, H))),
        "two": striped(np.random.permutation(T)[:S]),
        "k2": striped8(np.random.randint(0, G, (8, H))),
        "n1": striped(perm[:W]),
        "n2": striped(perm[W:]),
        "k3": striped8(np.random.randint(0, G, (8, H))),
        "k4": striped8(np.random.randint(0, G, (8, H))),
        "duo": striped(np.random.permutation(T)[:S]),
        "k5": striped8(np.random.randint(0, G, (8, H))),
        "hz": striped8(np.random.randint(0, T, (8, S))),
        "n3": striped(perm2[:W]),
        "n4": striped(perm2[W:]),
        "n5": striped(perm3[:W]),
        "n6": striped(perm3[W:]),
    }


def reference(x_words, x_scales, d_words, d_scales, gs, offs, k1, two, k2, n1, n2, k3, k4, duo, k5, hz, n3, n4, n5, n6):
    d_k3 = unpack_weight(d_words, d_scales)[np.arange(K)[:, None], runs(k3, K)]
    d_k1 = unpack_weight(d_words, d_scales)[np.arange(K)[:, None], runs(k1, K)]
    xq = unpack_weight(x_words, x_scales)[:, unstriped(offs)]
    d_k2 = unpack_weight(d_words, d_scales)[np.arange(K)[:, None], runs(k2, K)]
    x_two = unpack_weight(x_words, x_scales)[:, unstriped(two)]
    h = 0.0625 * (d_k1.T @ xq + d_k2.T @ x_two)
    pa = h[:, unstriped(n1)]
    pb = h[:, unstriped(n2)]
    rb = np.maximum(pa, pb)
    ra = pa / (np.abs(pb) + 0.5)
    ua = np.zeros((H, S))
    ua[:, unstriped(n1)] = ra
    ub = ua.copy()
    ub[:, unstriped(n2)] = rb
    z = f64(gs) * ub
    d_k4 = unpack_weight(d_words, d_scales)[np.arange(K)[:, None], runs(k4, K)]
    x_duo = unpack_weight(x_words, x_scales)[:, unstriped(duo)]
    d_k5 = unpack_weight(d_words, d_scales)[np.arange(K)[:, None], runs(k5, K)]
    x_hz = unpack_weight(x_words, x_scales)[np.arange(K)[:, None], runs(hz, K)]
    h2 = 0.0625 * ((d_k3.T @ mxq(z, 0, "e4m3") + d_k4.T @ x_duo + d_k5.T @ x_hz))
    pa2 = h2[:, unstriped(n3)]
    pb2 = h2[:, unstriped(n4)]
    rb2 = np.minimum(pa2, pb2)
    ra2 = np.maximum(pa2, pb2)
    ua2 = np.zeros((H, S))
    ua2[:, unstriped(n5)] = ra2
    ub2 = ua2.copy()
    ub2[:, unstriped(n6)] = rb2
    out_0 = ub2 - h2
    return (out_0,) + planes(out_0)

@@ -1,0 +1,305 @@
+from contextlib import ExitStack
+
+import concourse.mybir as mybir
+from concourse.masks import make_identity
+
+K, T, S, G, H, W = 512, 1024, 256, 2048, 512, 128
+FLOPS = 5 * 2 * K * H * S
+
+F32 = mybir.dt.float32
+BF16 = mybir.dt.bfloat16
+I32 = mybir.dt.int32
+U32 = mybir.dt.uint32
+U16 = mybir.dt.uint16
+U8 = mybir.dt.uint8
+FP8X4 = mybir.dt.float8_e4m3fn_x4
+ALU = mybir.AluOpType
+ACT = mybir.ActivationFunctionType
+
+P = 128
+HALF = 256
+
+
+def tile_picked_mttzmthratiocpor_none_po_kernel(
+    tc, x_words, x_scales, d_words, d_scales, gs, offs, k1, two, k2, n1, n2, k3, k4, duo, k5, hz,
+    n3, n4, n5, n6, out_0, out_1, out_2,
+):
+    nc = tc.nc
+    with ExitStack() as ctx:
+        lists = ctx.enter_context(tc.tile_pool(name="lists", bufs=1))
+        pool = ctx.enter_context(tc.tile_pool(name="work", bufs=1))
+        psum = ctx.enter_context(tc.psum_pool(name="psum", bufs=1))
+
+        def sbuf(shape, dtype, name, tag=None):
+            return pool.tile(shape, dtype, name=name, tag=tag or name, align_bytes=64)
+
+        def load_list(src, name):
+            tile = lists.tile(list(src.shape), U16, name=name)
+            nc.sync.dma_start(tile[:], src)
+            return tile
+
+        def load_scales(src, name):
+            tile = sbuf([P, src.shape[2]], U8, name)
+            rows = src[0].bitcast(I32)
+            nc.sync.dma_start(tile[:].bitcast(I32), rows.unsqueeze(1).to_broadcast([16, 8, rows.shape[1]]))
+            return tile
+
+        def load_words(src, name):
+            tile = sbuf([P, src.shape[2]], U32, name)
+            nc.sync.dma_start(tile[:].bitcast(I32), src[0].rearrange("p n t -> p (n t)").bitcast(I32))
+            return tile
+
+        x_sc = load_scales(x_scales, "x_sc")
+        l_offs = load_list(offs, "l_offs")
+        l_two = load_list(two, "l_two")
+        d_sc = load_scales(d_scales, "d_sc")
+        l_k1 = load_list(k1, "l_k1")
+        l_k2 = load_list(k2, "l_k2")
+        x_w = load_words(x_words, "x_w")
+        d_w = load_words(d_words, "d_w")
+        l_n2 = load_list(n2, "l_n2")
+        l_n1 = load_list(n1, "l_n1")
+        gain = sbuf([P, 4], F32, "gain")
+        with nc.allow_non_contiguous_dma(reason="one weight a row"):
+            nc.gpsimd.dma_start(gain[:], gs.rearrange("(b p) o -> p (b o)", p=P))
+        l_k4 = load_list(k4, "l_k4")
+        l_k5 = load_list(k5, "l_k5")
+        l_k3 = load_list(k3, "l_k3")
+        l_duo = load_list(duo, "l_duo")
+        l_hz = load_list(hz, "l_hz")
+        l_n3 = load_list(n3, "l_n3")
+        l_n4 = load_list(n4, "l_n4")
+        l_n5 = load_list(n5, "l_n5")
+        l_n6 = load_list(n6, "l_n6")
+
+        ident = sbuf([P, P], F32, "ident")
+        make_identity(nc, ident[:])
+        neg_gain = sbuf([P, 4], F32, "neg_gain")
+        nc.gpsimd.tensor_scalar(neg_gain[:], gain[:], -1.0, 0.0, ALU.mult, ALU.add)
+
+        def plane(name, pieces):
+            tile = sbuf([P, pieces * HALF], U8, name)
+            nc.vector.memset(tile[:].bitcast(I32), 0)
+            return tile
+
+        plane_1a = plane("plane_1a", 4)
+        plane_1b = plane("plane_1b", 2)
+        plane_2a = plane("plane_2a", 5)
+        plane_2b = plane("plane_2b", 3)
+
+        def part(lst, half):
+            return lst[:, half * 16 : (half + 1) * 16]
+
+        def gather(name, dtype, picks, tag=None):
+            tile = sbuf([P, len(picks) * HALF], dtype, name, tag)
+            for n, (window, offsets) in enumerate(picks):
+                nc.vector.tensor_copy(tile[:, n * HALF : (n + 1) * HALF], window[:].indirect(offsets))
+            return tile
+
+        def gather_scales(name, picks, target, queue, tag=None):
+            tile = gather(name, U8, picks, tag)
+            for i in range(4):
+                queue.dma_start(target[i:P:32, :].bitcast(I32), tile[8 * i : P : 32, :].bitcast(I32))
+
+        def piece(tile, n):
+            return tile[:, n * HALF : (n + 1) * HALF]
+
+        def product(acc, j, weights, tokens, start, stop):
+            cols = slice(j * P, (j + 1) * P)
+            nc.tensor.matmul_mx(
+                out=acc[:],
+                lhsT=weights[0][:, cols].bitcast(FP8X4), lhsT_scale=weights[1][:, cols],
+                rhs=tokens[0].bitcast(FP8X4), rhs_scale=tokens[1],
+                start=start, stop=stop,
+            )
+
+        def bank(name, tag, bufs, shape):
+            return psum.tile(shape, F32, name=name, tag=tag, bufs=bufs)
+
+        def fetch(out, window, lst):
+            nc.scalar.activation(out, window[:].indirect(lst[:]), ACT.Copy)
+
+        def put(window, lst, values):
+            nc.scalar.activation(window[:].indirect(lst[:]), values, ACT.Copy)
+
+        def turn_rows(rows, turned, b):
+            dst = turned[:].rearrange("c (h u m e) -> c h u m e", h=2, u=2, e=2)[:, :, :, 32 * b : 32 * (b + 1), :]
+            if b < 3:
+                t1 = bank("t1", "t1", 2, [P, 2, P])
+                for h in range(2):
+                    nc.tensor.transpose(t1[:, h, :], rows[:, h * P : (h + 1) * P], ident[:])
+                nc.vector.tensor_copy(dst, t1[:].rearrange("c h (m u e) -> c h u m e", u=2, e=2))
+            else:
+                for h, (tag, copy) in enumerate((("t1", nc.scalar.copy), ("t2", nc.vector.tensor_copy))):
+                    t1 = bank("t1_last", tag, 2, [P, P])
+                    nc.tensor.transpose(t1[:], rows[:, h * P : (h + 1) * P], ident[:])
+                    copy(dst[:, h], t1[:].rearrange("c (m u e) -> c u m e", u=2, e=2))
+
+        def quantise(turned, name):
+            grouped = sbuf([P, 4 * S], BF16, name + "_grouped")
+            codes = sbuf([P, S], U32, name + "_codes")
+            scales = sbuf([P, S], U8, name + "_scales")
+            words = turned[:].bitcast(F32)
+            for h, (tag, copy) in enumerate((("t1", nc.scalar.copy), ("t2", nc.vector.tensor_copy))):
+                t2 = bank("t2", tag, 2, [P, 2, P])
+                for u in range(2):
+                    nc.tensor.transpose(t2[:, u, :], words[:, (2 * h + u) * P : (2 * h + u + 1) * P], ident[:])
+                dst = grouped[:].bitcast(F32)[:, h * 2 * P : (h + 1) * 2 * P].rearrange("p (c u) -> p c u", u=2)
+                copy(dst, t2[:].rearrange("p u c -> p c u"))
+            for h in range(2):
+                cols = slice(h * P, (h + 1) * P)
+                nc.vector.quantize_mx(
+                    out=codes[:, cols].bitcast(FP8X4), scales=scales[:, cols], in_=grouped[:, h * 4 * P : (h + 1) * 4 * P]
+                )
+            return codes, scales
+
+        gather_scales("s_1a", [(x_sc, l_offs[:]), (x_sc, l_two[:]), (d_sc, part(l_k1, 0)), (d_sc, part(l_k2, 0))], plane_1a, nc.scalar)
+        w_x1 = gather("w_x1", U32, [(x_w, l_offs[:]), (x_w, l_two[:])])
+        w_1a = gather("w_1a", U32, [(d_w, part(l_k1, 0)), (d_w, part(l_k2, 0))])
+        gather_scales("s_1b", [(d_sc, part(l_k1, 1)), (d_sc, part(l_k2, 1))], plane_1b, nc.sync, tag="s_1a")
+        w_1b = gather("w_1b", U32, [(d_w, part(l_k1, 1)), (d_w, part(l_k2, 1))])
+        x_offs = (piece(w_x1, 0), piece(plane_1a, 0))
+        x_two = (piece(w_x1, 1), piece(plane_1a, 1))
+        first = [
+            [(piece(w_1a, n), piece(plane_1a, 2 + n)) for n in range(2)],
+            [(piece(w_1b, n), piece(plane_1b, n)) for n in range(2)],
+        ]
+
+        w_45a = gather("w_45a", U32, [(d_w, part(l_k4, 0)), (d_w, part(l_k5, 0))])
+
+        def ratio_fetch(half):
+            name = "r%d_" % half
+            pa = sbuf([P, 2, W], F32, name + "pa")
+            pb = sbuf([P, 2, W], F32, name + "pb")
+            for j in range(2):
+                acc = bank("acc", "acc", 4, [P, S])
+                product(acc, j, first[half][0], x_offs, True, False)
+                product(acc, j, first[half][1], x_two, False, True)
+                h = sbuf([P, S], F32, name + "h%d" % j)
+                nc.scalar.activation(h[:], acc[:], ACT.Copy, scale=0.0625)
+                fetch(pb[:, j, :], h, l_n2)
+                fetch(pa[:, j, :], h, l_n1)
+            size = sbuf([P, 2, W], F32, name + "size")
+            seed = sbuf([P, 2, W], F32, name + "seed")
+            nc.scalar.activation(size[:], pb[:], ACT.Abs)
+            nc.scalar.activation(seed[:], size[:], ACT.Abs_reciprocal_sqrt, bias=0.5)
+            return pa, pb, size, seed
+
+        def ratio_factors(half, pa, pb, size, seed):
+            name = "r%d_" % half
+            larger = sbuf([P, 2, W], F32, name + "larger")
+            rb = sbuf([P, 2, W], F32, name + "rb")
+            nc.vector.tensor_tensor(larger[:], pa[:], pb[:], ALU.max)
+            for j in range(2):
+                b = 2 * half + j
+                nc.vector.tensor_scalar(rb[:, j, :], larger[:, j, :], gain[:, b : b + 1], None, ALU.mult)
+            guess = sbuf([P, 2, W], F32, name + "guess")
+            near_one = sbuf([P, 2, W], F32, name + "near_one")
+            rough = sbuf([P, 2, W], F32, name + "rough")
+            nc.vector.tensor_tensor(guess[:], seed[:], seed[:], ALU.mult)
+            nc.vector.scalar_tensor_tensor(near_one[:], size[:], 0.5, guess[:], ALU.add, ALU.mult)
+            for j in range(2):
+                b = 2 * half + j
+                nc.vector.scalar_tensor_tensor(rough[:, j, :], pa[:, j, :], neg_gain[:, b : b + 1], guess[:, j, :], ALU.mult, ALU.mult)
+            return rb, near_one, rough
+
+        def ratio(half, near_one, rough, tag):
+            ra = sbuf([P, 2, W], F32, "r%d_ra" % half, tag)
+            nc.vector.scalar_tensor_tensor(ra[:], near_one[:], 2.0, rough[:], ALU.subtract, ALU.mult)
+            return ra
+
+        z = [sbuf([P, S], F32, "z%d" % b) for b in range(4)]
+
+        def put_pair(half, lst, values):
+            for j in range(2):
+                put(z[2 * half + j], lst, values[:, j, :])
+
+        rb, near_one, rough = ratio_factors(0, *ratio_fetch(0))
+        put_pair(0, l_n2, rb)
+        gather_scales(
+            "s_2a",
+            [(d_sc, part(l_k3, 0)), (d_sc, part(l_k4, 0)), (d_sc, part(l_k5, 0)), (x_sc, l_duo[:]), (x_sc, l_hz[:])],
+            plane_2a, nc.sync, tag="r0_guess",
+        )
+        fetched = ratio_fetch(1)
+        put_pair(0, l_n1, ratio(0, near_one, rough, "r1_h1"))
+        rb, near_one, rough = ratio_factors(1, *fetched)
+        ra = ratio(1, near_one, rough, None)
+        put_pair(1, l_n2, rb)
+        put_pair(1, l_n1, ra)
+        z_turned = sbuf([P, 4 * S], BF16, "z_turned", tag="r1_near_one")
+        for b in range(4):
+            turn_rows(z[b], z_turned, b)
+        w_x2 = gather("w_x2", U32, [(x_w, l_duo[:]), (x_w, l_hz[:])], tag="r1_rough")
+        w_3a = gather("w_3a", U32, [(d_w, part(l_k3, 0))], tag="z2")
+        gather_scales(
+            "s_2b", [(d_sc, part(l_k3, 1)), (d_sc, part(l_k4, 1)), (d_sc, part(l_k5, 1))], plane_2b, nc.sync, tag="z3"
+        )
+        z_codes, z_scales = quantise(z_turned, "z")
+        w_4b = gather("w_4b", U32, [(d_w, part(l_k4, 1))], tag="z_grouped")
+
+        x_duo = (piece(w_x2, 0), piece(plane_2a, 3))
+        x_hz = (piece(w_x2, 1), piece(plane_2a, 4))
+        z_mx = (z_codes[:], z_scales[:])
+        out_turned = sbuf([P, 4 * S], BF16, "out_turned")
+
+        def sort_fetch(half, m3, m4, m5):
+            name = "s%d_" % half
+            pa = sbuf([P, 2, W], F32, name + "pa")
+            pb = sbuf([P, 2, W], F32, name + "pb")
+            larger = sbuf([P, 2, W], F32, name + "larger")
+            smaller = sbuf([P, 2, W], F32, name + "smaller")
+            h2 = []
+            for j in range(2):
+                acc = bank("acc", "acc", 4, [P, S])
+                product(acc, j, m4, x_duo, True, False)
+                product(acc, j, m5, x_hz, False, False)
+                product(acc, j, m3, z_mx, False, True)
+                h = sbuf([P, S], F32, name + "h%d" % j)
+                if half == 0 and j == 0:
+                    nc.scalar.activation(h[:], acc[:], ACT.Copy, scale=0.0625)
+                else:
+                    nc.vector.tensor_scalar(h[:], acc[:], 0.0625, None, ALU.mult)
+                fetch(pa[:, j, :], h, l_n3)
+                fetch(pb[:, j, :], h, l_n4)
+                h2.append(h)
+                nc.vector.tensor_tensor(larger[:, j, :], pa[:, j, :], pb[:, j, :], ALU.max)
+                nc.vector.tensor_tensor(smaller[:, j, :], pa[:, j, :], pb[:, j, :], ALU.min)
+            return h2, larger, smaller
+
+        def sort_put(half, larger, smaller):
+            name = "s%d_" % half
+            ub2 = [sbuf([P, S], F32, name + "u%d" % j) for j in range(2)]
+            for j in range(2):
+                put(ub2[j], l_n5, larger[:, j, :])
+            for j in range(2):
+                put(ub2[j], l_n6, smaller[:, j, :])
+            return ub2
+
+        def finish(half, h2, ub2, tag):
+            y = sbuf([P, 2, S], F32, "y%d" % half, tag)
+            for j in range(2):
+                b = 2 * half + j
+                nc.vector.tensor_tensor(y[:, j, :], ub2[j][:], h2[j][:], ALU.subtract)
+                nc.sync.dma_start(out_0[b * P : (b + 1) * P, :], y[:, j, :])
+                turn_rows(y[:, j, :], out_turned, b)
+
+        h2_0, larger, smaller = sort_fetch(
+            0, (w_3a[:], piece(plane_2a, 0)), (piece(w_45a, 0), piece(plane_2a, 1)), (piece(w_45a, 1), piece(plane_2a, 2))
+        )
+        w_2b = gather("w_2b", U32, [(d_w, part(l_k5, 1)), (d_w, part(l_k3, 1))], tag="s0_pa")
+        ub2_0 = sort_put(0, larger, smaller)
+        h2_1, larger, smaller = sort_fetch(
+            1, (piece(w_2b, 1), piece(plane_2b, 0)), (w_4b[:], piece(plane_2b, 1)), (piece(w_2b, 0), piece(plane_2b, 2))
+        )
+        finish(0, h2_0, ub2_0, "s0_pa")
+        ub2_1 = sort_put(1, larger, smaller)
+        finish(1, h2_1, ub2_1, None)
+
+        y_codes, y_scales = quantise(out_turned, "y")
+        for h in range(2):
+            cols = slice(h * P, (h + 1) * P)
+            nc.sync.dma_start(out_1[0].rearrange("p n t -> p (n t)").bitcast(I32)[:, cols], y_codes[:, cols].bitcast(I32))
+        for i in range(4):
+            queue = nc.scalar if i % 2 == 0 else nc.sync
+            queue.dma_start(out_2[0][i:16:4, :].bitcast(I32), y_scales[i:P:32, :].bitcast(I32))

@@ -72,6 +72,9 @@ def tile_picked_mttzmthratiocpor_none_po_kernel(
         l_n5 = load_list(n5, "l_n5")
         l_n6 = load_list(n6, "l_n6")
 
+        warm = sbuf([P, 2], F32, "warm")
+        nc.vector.memset(warm[:, 0:1], 1.0)
+        nc.scalar.activation(warm[:, 1:2], warm[:, 0:1], ACT.Abs_reciprocal_sqrt)
         ident = sbuf([P, P], F32, "ident")
         make_identity(nc, ident[:])
         neg_gain = sbuf([P, 4], F32, "neg_gain")

@@ -59,9 +59,6 @@ def tile_picked_mttzmthratiocpor_none_po_kernel(
         d_w = load_words(d_words, "d_w")
         l_n2 = load_list(n2, "l_n2")
         l_n1 = load_list(n1, "l_n1")
-        gain = sbuf([P, 4], F32, "gain")
-        with nc.allow_non_contiguous_dma(reason="one weight a row"):
-            nc.gpsimd.dma_start(gain[:], gs.rearrange("(b p) o -> p (b o)", p=P))
         l_k4 = load_list(k4, "l_k4")
         l_k5 = load_list(k5, "l_k5")
         l_k3 = load_list(k3, "l_k3")
@@ -77,8 +74,6 @@ def tile_picked_mttzmthratiocpor_none_po_kernel(
         nc.scalar.activation(warm[:, 1:2], warm[:, 0:1], ACT.Abs_reciprocal_sqrt)
         ident = sbuf([P, P], F32, "ident")
         make_identity(nc, ident[:])
-        neg_gain = sbuf([P, 4], F32, "neg_gain")
-        nc.gpsimd.tensor_scalar(neg_gain[:], gain[:], -1.0, 0.0, ALU.mult, ALU.add)
 
         def plane(name, pieces):
             tile = sbuf([P, pieces * HALF], U8, name)
@@ -87,7 +82,9 @@ def tile_picked_mttzmthratiocpor_none_po_kernel(
 
         plane_1a = plane("plane_1a", 4)
         plane_1b = plane("plane_1b", 2)
-        plane_2a = plane("plane_2a", 5)
+        plane_4a = plane("plane_4a", 1)
+        plane_2a = plane("plane_2a", 3)
+        plane_hz = plane("plane_hz", 1)
         plane_2b = plane("plane_2b", 3)
 
         def part(lst, half):
@@ -116,8 +113,8 @@ def tile_picked_mttzmthratiocpor_none_po_kernel(
                 start=start, stop=stop,
             )
 
-        def bank(name, tag, bufs, shape):
-            return psum.tile(shape, F32, name=name, tag=tag, bufs=bufs)
+        def bank(name, number, shape):
+            return psum.tile(shape, F32, name=name, tag="bank%d" % number)
 
         def fetch(out, window, lst):
             nc.scalar.activation(out, window[:].indirect(lst[:]), ACT.Copy)
@@ -125,34 +122,56 @@ def tile_picked_mttzmthratiocpor_none_po_kernel(
         def put(window, lst, values):
             nc.scalar.activation(window[:].indirect(lst[:]), values, ACT.Copy)
 
-        def turn_rows(rows, turned, b):
-            dst = turned[:].rearrange("c (h u m e) -> c h u m e", h=2, u=2, e=2)[:, :, :, 32 * b : 32 * (b + 1), :]
-            if b < 3:
-                t1 = bank("t1", "t1", 2, [P, 2, P])
+        def turned_view(turned, b):
+            return turned[:].rearrange("c (h u m e) -> c h u m e", h=2, u=2, e=2)[:, :, :, 32 * b : 32 * (b + 1), :]
+
+        def turn_sum(target, terms, h):
+            for n, term in enumerate(terms):
+                nc.tensor.matmul(
+                    target, term[:, h * P : (h + 1) * P], ident[:],
+                    start=(n == 0), stop=(n == len(terms) - 1), is_transpose=True,
+                )
+
+        def turn_rows(terms, turned, b, copy):
+            t1 = bank("t1", 6 + b % 2, [P, 2, P])
+            for h in range(2):
+                turn_sum(t1[:, h, :], terms, h)
+            copy(turned_view(turned, b), t1[:].rearrange("c h (m u e) -> c h u m e", u=2, e=2))
+
+        def turn_last_rows(terms, turned):
+            t1 = [bank("t1_last", 2 + h, [P, P]) for h in range(2)]
+            for n, term in enumerate(terms):
                 for h in range(2):
-                    nc.tensor.transpose(t1[:, h, :], rows[:, h * P : (h + 1) * P], ident[:])
-                nc.vector.tensor_copy(dst, t1[:].rearrange("c h (m u e) -> c h u m e", u=2, e=2))
-            else:
-                for h, (tag, copy) in enumerate((("t1", nc.scalar.copy), ("t2", nc.vector.tensor_copy))):
-                    t1 = bank("t1_last", tag, 2, [P, P])
-                    nc.tensor.transpose(t1[:], rows[:, h * P : (h + 1) * P], ident[:])
-                    copy(dst[:, h], t1[:].rearrange("c (m u e) -> c u m e", u=2, e=2))
+                    nc.tensor.matmul(
+                        t1[h][:], term[:, h * P : (h + 1) * P], ident[:], start=(n == 0), stop=(n == 1), is_transpose=True
+                    )
+            for h, copy in enumerate((nc.scalar.copy, nc.vector.tensor_copy)):
+                copy(turned_view(turned, 3)[:, h], t1[h][:].rearrange("c (m u e) -> c u m e", u=2, e=2))
+
+        def turn_rows_weighted(rows, turned, b, gain):
+            dst = turned[:].rearrange("c (h u m e) -> c h u m e", h=2, u=2, e=2)[:, :, :, 32 * b : 32 * (b + 1), :]
+            weight = gain[:, b * P : (b + 1) * P].rearrange("c (m u e) -> c u m e", u=2, e=2)
+            t1 = bank("t1", 2 + b % 2, [P, 2, P])
+            for h in range(2):
+                nc.tensor.transpose(t1[:, h, :], rows[:, h * P : (h + 1) * P], ident[:])
+            for h in range(2):
+                nc.vector.tensor_tensor(dst[:, h], t1[:, h, :].rearrange("c (m u e) -> c u m e", u=2, e=2), weight, ALU.mult)
 
         def quantise(turned, name):
-            grouped = sbuf([P, 4 * S], BF16, name + "_grouped")
+            grouped = [sbuf([P, 4 * P], BF16, name + "_grouped%d" % h) for h in range(2)]
             codes = sbuf([P, S], U32, name + "_codes")
             scales = sbuf([P, S], U8, name + "_scales")
             words = turned[:].bitcast(F32)
-            for h, (tag, copy) in enumerate((("t1", nc.scalar.copy), ("t2", nc.vector.tensor_copy))):
-                t2 = bank("t2", tag, 2, [P, 2, P])
+            for h, (tag, copy) in enumerate(((6, nc.scalar.copy), (7, nc.vector.tensor_copy))):
+                t2 = bank("t2", tag, [P, 2, P])
                 for u in range(2):
                     nc.tensor.transpose(t2[:, u, :], words[:, (2 * h + u) * P : (2 * h + u + 1) * P], ident[:])
-                dst = grouped[:].bitcast(F32)[:, h * 2 * P : (h + 1) * 2 * P].rearrange("p (c u) -> p c u", u=2)
+                dst = grouped[h][:].bitcast(F32).rearrange("p (c u) -> p c u", u=2)
                 copy(dst, t2[:].rearrange("p u c -> p c u"))
             for h in range(2):
                 cols = slice(h * P, (h + 1) * P)
                 nc.vector.quantize_mx(
-                    out=codes[:, cols].bitcast(FP8X4), scales=scales[:, cols], in_=grouped[:, h * 4 * P : (h + 1) * 4 * P]
+                    out=codes[:, cols].bitcast(FP8X4), scales=scales[:, cols], in_=grouped[h][:]
                 )
             return codes, scales
 
@@ -160,26 +179,22 @@ def tile_picked_mttzmthratiocpor_none_po_kernel(
         w_x1 = gather("w_x1", U32, [(x_w, l_offs[:]), (x_w, l_two[:])])
         w_1a = gather("w_1a", U32, [(d_w, part(l_k1, 0)), (d_w, part(l_k2, 0))])
         gather_scales("s_1b", [(d_sc, part(l_k1, 1)), (d_sc, part(l_k2, 1))], plane_1b, nc.sync, tag="s_1a")
-        w_1b = gather("w_1b", U32, [(d_w, part(l_k1, 1)), (d_w, part(l_k2, 1))])
         x_offs = (piece(w_x1, 0), piece(plane_1a, 0))
         x_two = (piece(w_x1, 1), piece(plane_1a, 1))
-        first = [
-            [(piece(w_1a, n), piece(plane_1a, 2 + n)) for n in range(2)],
-            [(piece(w_1b, n), piece(plane_1b, n)) for n in range(2)],
-        ]
 
-        w_45a = gather("w_45a", U32, [(d_w, part(l_k4, 0)), (d_w, part(l_k5, 0))])
 
-        def ratio_fetch(half):
+        def ratio_fetch(half, m1, m2):
             name = "r%d_" % half
             pa = sbuf([P, 2, W], F32, name + "pa")
             pb = sbuf([P, 2, W], F32, name + "pb")
+            accs = [bank("acc", 2 * half + j, [P, S]) for j in range(2)]
             for j in range(2):
-                acc = bank("acc", "acc", 4, [P, S])
-                product(acc, j, first[half][0], x_offs, True, False)
-                product(acc, j, first[half][1], x_two, False, True)
+                product(accs[j], j, m1, x_offs, True, False)
+            for j in range(2):
+                product(accs[j], j, m2, x_two, False, True)
+            for j in range(2):
                 h = sbuf([P, S], F32, name + "h%d" % j)
-                nc.scalar.activation(h[:], acc[:], ACT.Copy, scale=0.0625)
+                nc.scalar.activation(h[:], accs[j][:], ACT.Copy, scale=0.0625)
                 fetch(pb[:, j, :], h, l_n2)
                 fetch(pa[:, j, :], h, l_n1)
             size = sbuf([P, 2, W], F32, name + "size")
@@ -188,22 +203,23 @@ def tile_picked_mttzmthratiocpor_none_po_kernel(
             nc.scalar.activation(seed[:], size[:], ACT.Abs_reciprocal_sqrt, bias=0.5)
             return pa, pb, size, seed
 
+        gain = sbuf([P, H], F32, "gain", tag="s_1a")
+        nc.gpsimd.dma_start(gain[:], gs.rearrange("k o -> (k o)").partition_broadcast(P))
+        z = [sbuf([P, S], F32, "z%d" % b) for b in range(4)]
+
         def ratio_factors(half, pa, pb, size, seed):
             name = "r%d_" % half
-            larger = sbuf([P, 2, W], F32, name + "larger")
             rb = sbuf([P, 2, W], F32, name + "rb")
-            nc.vector.tensor_tensor(larger[:], pa[:], pb[:], ALU.max)
-            for j in range(2):
-                b = 2 * half + j
-                nc.vector.tensor_scalar(rb[:, j, :], larger[:, j, :], gain[:, b : b + 1], None, ALU.mult)
+            nc.vector.tensor_tensor(rb[:], pa[:], pb[:], ALU.max)
             guess = sbuf([P, 2, W], F32, name + "guess")
             near_one = sbuf([P, 2, W], F32, name + "near_one")
             rough = sbuf([P, 2, W], F32, name + "rough")
-            nc.vector.tensor_tensor(guess[:], seed[:], seed[:], ALU.mult)
-            nc.vector.scalar_tensor_tensor(near_one[:], size[:], 0.5, guess[:], ALU.add, ALU.mult)
             for j in range(2):
-                b = 2 * half + j
-                nc.vector.scalar_tensor_tensor(rough[:, j, :], pa[:, j, :], neg_gain[:, b : b + 1], guess[:, j, :], ALU.mult, ALU.mult)
+                nc.vector.tensor_tensor(guess[:, j, :], seed[:, j, :], seed[:, j, :], ALU.mult)
+            for j in range(2):
+                nc.vector.scalar_tensor_tensor(near_one[:, j, :], size[:, j, :], 0.5, guess[:, j, :], ALU.add, ALU.mult)
+            for j in range(2):
+                nc.vector.scalar_tensor_tensor(rough[:, j, :], pa[:, j, :], -1.0, guess[:, j, :], ALU.mult, ALU.mult)
             return rb, near_one, rough
 
         def ratio(half, near_one, rough, tag):
@@ -211,38 +227,40 @@ def tile_picked_mttzmthratiocpor_none_po_kernel(
             nc.vector.scalar_tensor_tensor(ra[:], near_one[:], 2.0, rough[:], ALU.subtract, ALU.mult)
             return ra
 
-        z = [sbuf([P, S], F32, "z%d" % b) for b in range(4)]
-
         def put_pair(half, lst, values):
             for j in range(2):
                 put(z[2 * half + j], lst, values[:, j, :])
 
-        rb, near_one, rough = ratio_factors(0, *ratio_fetch(0))
+        fetched = ratio_fetch(0, *[(piece(w_1a, n), piece(plane_1a, 2 + n)) for n in range(2)])
+        w_1b = gather("w_1b", U32, [(d_w, part(l_k1, 1)), (d_w, part(l_k2, 1)), (d_w, part(l_k4, 0))], tag="w_1a")
+        rb, near_one, rough = ratio_factors(0, *fetched)
         put_pair(0, l_n2, rb)
+        gather_scales("s_4a", [(d_sc, part(l_k4, 0))], plane_4a, nc.sync, tag="r0_pb")
         gather_scales(
             "s_2a",
-            [(d_sc, part(l_k3, 0)), (d_sc, part(l_k4, 0)), (d_sc, part(l_k5, 0)), (x_sc, l_duo[:]), (x_sc, l_hz[:])],
+            [(d_sc, part(l_k5, 0)), (d_sc, part(l_k3, 0)), (x_sc, l_duo[:])],
             plane_2a, nc.sync, tag="r0_guess",
         )
-        fetched = ratio_fetch(1)
+        fetched = ratio_fetch(1, *[(piece(w_1b, n), piece(plane_1b, n)) for n in range(2)])
         put_pair(0, l_n1, ratio(0, near_one, rough, "r1_h1"))
         rb, near_one, rough = ratio_factors(1, *fetched)
         ra = ratio(1, near_one, rough, None)
         put_pair(1, l_n2, rb)
         put_pair(1, l_n1, ra)
         z_turned = sbuf([P, 4 * S], BF16, "z_turned", tag="r1_near_one")
-        for b in range(4):
-            turn_rows(z[b], z_turned, b)
-        w_x2 = gather("w_x2", U32, [(x_w, l_duo[:]), (x_w, l_hz[:])], tag="r1_rough")
-        w_3a = gather("w_3a", U32, [(d_w, part(l_k3, 0))], tag="z2")
-        gather_scales(
-            "s_2b", [(d_sc, part(l_k3, 1)), (d_sc, part(l_k4, 1)), (d_sc, part(l_k5, 1))], plane_2b, nc.sync, tag="z3"
-        )
+        for b in range(2):
+            turn_rows_weighted(z[b], z_turned, b, gain)
+        gather_scales("s_hz", [(x_sc, l_hz[:])], plane_hz, nc.sync, tag="r1_guess")
+        w_2a = gather("w_2a", U32, [(x_w, l_duo[:]), (x_w, l_hz[:]), (d_w, part(l_k5, 0))], tag="r1_rough")
+        for b in range(2, 4):
+            turn_rows_weighted(z[b], z_turned, b, gain)
+        w_3a = gather("w_3a", U32, [(d_w, part(l_k3, 0))], tag="s_1a")
         z_codes, z_scales = quantise(z_turned, "z")
-        w_4b = gather("w_4b", U32, [(d_w, part(l_k4, 1))], tag="z_grouped")
+        gather_scales("s_2b", [(d_sc, part(l_k4, 1)), (d_sc, part(l_k5, 1)), (d_sc, part(l_k3, 1))], plane_2b, nc.sync, tag="z_grouped0")
+        w_4b = gather("w_4b", U32, [(d_w, part(l_k4, 1))], tag="z_grouped1")
 
-        x_duo = (piece(w_x2, 0), piece(plane_2a, 3))
-        x_hz = (piece(w_x2, 1), piece(plane_2a, 4))
+        x_duo = (piece(w_2a, 0), piece(plane_2a, 2))
+        x_hz = (piece(w_2a, 1), plane_hz[:])
         z_mx = (z_codes[:], z_scales[:])
         out_turned = sbuf([P, 4 * S], BF16, "out_turned")
 
@@ -253,13 +271,14 @@ def tile_picked_mttzmthratiocpor_none_po_kernel(
             larger = sbuf([P, 2, W], F32, name + "larger")
             smaller = sbuf([P, 2, W], F32, name + "smaller")
             h2 = []
+            accs = [bank("acc", 4 * half + j, [P, S]) for j in range(2)]
+            for n, (weights, tokens) in enumerate(((m4, x_duo), (m5, x_hz), (m3, z_mx))):
+                for j in range(2):
+                    product(accs[j], j, weights, tokens, n == 0, n == 2)
             for j in range(2):
-                acc = bank("acc", "acc", 4, [P, S])
-                product(acc, j, m4, x_duo, True, False)
-                product(acc, j, m5, x_hz, False, False)
-                product(acc, j, m3, z_mx, False, True)
+                acc = accs[j]
                 h = sbuf([P, S], F32, name + "h%d" % j)
-                if half == 0 and j == 0:
+                if half == 0:
                     nc.scalar.activation(h[:], acc[:], ACT.Copy, scale=0.0625)
                 else:
                     nc.vector.tensor_scalar(h[:], acc[:], 0.0625, None, ALU.mult)
@@ -267,8 +286,8 @@ def tile_picked_mttzmthratiocpor_none_po_kernel(
                 fetch(pb[:, j, :], h, l_n4)
                 h2.append(h)
                 nc.vector.tensor_tensor(larger[:, j, :], pa[:, j, :], pb[:, j, :], ALU.max)
-                nc.vector.tensor_tensor(smaller[:, j, :], pa[:, j, :], pb[:, j, :], ALU.min)
-            return h2, larger, smaller
+            nc.vector.tensor_tensor(smaller[:], pa[:], pb[:], ALU.min)
+            return h2, larger, smaller, accs
 
         def sort_put(half, larger, smaller):
             name = "s%d_" % half
@@ -285,18 +304,25 @@ def tile_picked_mttzmthratiocpor_none_po_kernel(
                 b = 2 * half + j
                 nc.vector.tensor_tensor(y[:, j, :], ub2[j][:], h2[j][:], ALU.subtract)
                 nc.sync.dma_start(out_0[b * P : (b + 1) * P, :], y[:, j, :])
-                turn_rows(y[:, j, :], out_turned, b)
+            return y
 
-        h2_0, larger, smaller = sort_fetch(
-            0, (w_3a[:], piece(plane_2a, 0)), (piece(w_45a, 0), piece(plane_2a, 1)), (piece(w_45a, 1), piece(plane_2a, 2))
+        h2_0, larger, smaller, accs = sort_fetch(
+            0, (w_3a[:], piece(plane_2a, 1)), (piece(w_1b, 2), plane_4a[:]), (piece(w_2a, 2), piece(plane_2a, 0))
         )
-        w_2b = gather("w_2b", U32, [(d_w, part(l_k5, 1)), (d_w, part(l_k3, 1))], tag="s0_pa")
+        w_53b = gather("w_53b", U32, [(d_w, part(l_k5, 1)), (d_w, part(l_k3, 1))], tag="s0_pa")
         ub2_0 = sort_put(0, larger, smaller)
-        h2_1, larger, smaller = sort_fetch(
-            1, (piece(w_2b, 1), piece(plane_2b, 0)), (w_4b[:], piece(plane_2b, 1)), (piece(w_2b, 0), piece(plane_2b, 2))
+        h2_1, larger, smaller, accs = sort_fetch(
+            1, (piece(w_53b, 1), piece(plane_2b, 2)), (w_4b[:], piece(plane_2b, 0)), (piece(w_53b, 0), piece(plane_2b, 1))
         )
-        finish(0, h2_0, ub2_0, "s0_pa")
+        y = finish(0, h2_0, ub2_0, "s0_pa")
+        for j in range(2):
+            turn_rows([y[:, j, :]], out_turned, j, nc.vector.tensor_copy)
+        minus_h2 = sbuf([P, 2, S], F32, "minus_h2", tag="s1_pa")
+        for j in range(2):
+            nc.vector.tensor_scalar(minus_h2[:, j, :], accs[j][:], -0.0625, None, ALU.mult)
         ub2_1 = sort_put(1, larger, smaller)
+        turn_rows([minus_h2[:, 0, :], ub2_1[0]], out_turned, 2, nc.scalar.copy)
+        turn_last_rows([minus_h2[:, 1, :], ub2_1[1]], out_turned)
         finish(1, h2_1, ub2_1, None)
 
         y_codes, y_scales = quantise(out_turned, "y")

from contextlib import ExitStack

import concourse.mybir as mybir
from concourse.masks import make_identity

K, T, S, G, H, W = 512, 1024, 256, 2048, 512, 128
FLOPS = 5 * 2 * K * H * S

F32 = mybir.dt.float32
BF16 = mybir.dt.bfloat16
I32 = mybir.dt.int32
U32 = mybir.dt.uint32
U16 = mybir.dt.uint16
U8 = mybir.dt.uint8
FP8X4 = mybir.dt.float8_e4m3fn_x4
ALU = mybir.AluOpType
ACT = mybir.ActivationFunctionType

P = 128
HALF = 256


def tile_picked_mttzmthratiocpor_none_po_kernel(
    tc, x_words, x_scales, d_words, d_scales, gs, offs, k1, two, k2, n1, n2, k3, k4, duo, k5, hz,
    n3, n4, n5, n6, out_0, out_1, out_2,
):
    nc = tc.nc
    with ExitStack() as ctx:
        lists = ctx.enter_context(tc.tile_pool(name="lists", bufs=1))
        pool = ctx.enter_context(tc.tile_pool(name="work", bufs=1))
        psum = ctx.enter_context(tc.psum_pool(name="psum", bufs=1))

        def sbuf(shape, dtype, name, tag=None):
            return pool.tile(shape, dtype, name=name, tag=tag or name, align_bytes=64)

        def load_list(src, name):
            tile = lists.tile(list(src.shape), U16, name=name)
            nc.sync.dma_start(tile[:], src)
            return tile

        def load_scales(src, name):
            tile = sbuf([P, src.shape[2]], U8, name)
            rows = src[0].bitcast(I32)
            nc.sync.dma_start(tile[:].bitcast(I32), rows.unsqueeze(1).to_broadcast([16, 8, rows.shape[1]]))
            return tile

        def load_words(src, name):
            tile = sbuf([P, src.shape[2]], U32, name)
            nc.sync.dma_start(tile[:].bitcast(I32), src[0].rearrange("p n t -> p (n t)").bitcast(I32))
            return tile

        x_sc = load_scales(x_scales, "x_sc")
        l_offs = load_list(offs, "l_offs")
        l_two = load_list(two, "l_two")
        d_sc = load_scales(d_scales, "d_sc")
        l_k1 = load_list(k1, "l_k1")
        l_k2 = load_list(k2, "l_k2")
        x_w = load_words(x_words, "x_w")
        d_w = load_words(d_words, "d_w")
        l_n2 = load_list(n2, "l_n2")
        l_n1 = load_list(n1, "l_n1")
        l_k4 = load_list(k4, "l_k4")
        l_k5 = load_list(k5, "l_k5")
        l_k3 = load_list(k3, "l_k3")
        l_duo = load_list(duo, "l_duo")
        l_hz = load_list(hz, "l_hz")
        l_n3 = load_list(n3, "l_n3")
        l_n4 = load_list(n4, "l_n4")
        l_n5 = load_list(n5, "l_n5")
        l_n6 = load_list(n6, "l_n6")

        warm = sbuf([P, 2], F32, "warm")
        nc.vector.memset(warm[:, 0:1], 1.0)
        nc.scalar.activation(warm[:, 1:2], warm[:, 0:1], ACT.Abs_reciprocal_sqrt)
        ident = sbuf([P, P], F32, "ident")
        make_identity(nc, ident[:])

        def plane(name, pieces):
            tile = sbuf([P, pieces * HALF], U8, name)
            nc.vector.memset(tile[:].bitcast(I32), 0)
            return tile

        plane_1a = plane("plane_1a", 4)
        plane_1b = plane("plane_1b", 2)
        plane_4a = plane("plane_4a", 1)
        plane_2a = plane("plane_2a", 3)
        plane_hz = plane("plane_hz", 1)
        plane_2b = plane("plane_2b", 3)

        def part(lst, half):
            return lst[:, half * 16 : (half + 1) * 16]

        def gather(name, dtype, picks, tag=None):
            tile = sbuf([P, len(picks) * HALF], dtype, name, tag)
            for n, (window, offsets) in enumerate(picks):
                nc.vector.tensor_copy(tile[:, n * HALF : (n + 1) * HALF], window[:].indirect(offsets))
            return tile

        def gather_scales(name, picks, target, queue, tag=None):
            tile = gather(name, U8, picks, tag)
            for i in range(4):
                queue.dma_start(target[i:P:32, :].bitcast(I32), tile[8 * i : P : 32, :].bitcast(I32))

        def piece(tile, n):
            return tile[:, n * HALF : (n + 1) * HALF]

        def product(acc, j, weights, tokens, start, stop):
            cols = slice(j * P, (j + 1) * P)
            nc.tensor.matmul_mx(
                out=acc[:],
                lhsT=weights[0][:, cols].bitcast(FP8X4), lhsT_scale=weights[1][:, cols],
                rhs=tokens[0].bitcast(FP8X4), rhs_scale=tokens[1],
                start=start, stop=stop,
            )

        def bank(name, number, shape):
            return psum.tile(shape, F32, name=name, tag="bank%d" % number)

        def fetch(out, window, lst):
            nc.scalar.activation(out, window[:].indirect(lst[:]), ACT.Copy)

        def put(window, lst, values):
            nc.scalar.activation(window[:].indirect(lst[:]), values, ACT.Copy)

        def turned_view(turned, b):
            return turned[:].rearrange("c (h u m e) -> c h u m e", h=2, u=2, e=2)[:, :, :, 32 * b : 32 * (b + 1), :]

        def turn_sum(target, terms, h):
            for n, term in enumerate(terms):
                nc.tensor.matmul(
                    target, term[:, h * P : (h + 1) * P], ident[:],
                    start=(n == 0), stop=(n == len(terms) - 1), is_transpose=True,
                )

        def turn_rows(terms, turned, b, copy):
            t1 = bank("t1", 6 + b % 2, [P, 2, P])
            for h in range(2):
                turn_sum(t1[:, h, :], terms, h)
            copy(turned_view(turned, b), t1[:].rearrange("c h (m u e) -> c h u m e", u=2, e=2))

        def turn_last_rows(terms, turned):
            t1 = [bank("t1_last", 2 + h, [P, P]) for h in range(2)]
            for n, term in enumerate(terms):
                for h in range(2):
                    nc.tensor.matmul(
                        t1[h][:], term[:, h * P : (h + 1) * P], ident[:], start=(n == 0), stop=(n == 1), is_transpose=True
                    )
            for h, copy in enumerate((nc.scalar.copy, nc.vector.tensor_copy)):
                copy(turned_view(turned, 3)[:, h], t1[h][:].rearrange("c (m u e) -> c u m e", u=2, e=2))

        def turn_rows_weighted(rows, turned, b, gain):
            dst = turned[:].rearrange("c (h u m e) -> c h u m e", h=2, u=2, e=2)[:, :, :, 32 * b : 32 * (b + 1), :]
            weight = gain[:, b * P : (b + 1) * P].rearrange("c (m u e) -> c u m e", u=2, e=2)
            t1 = bank("t1", 2 + b % 2, [P, 2, P])
            for h in range(2):
                nc.tensor.transpose(t1[:, h, :], rows[:, h * P : (h + 1) * P], ident[:])
            for h in range(2):
                nc.vector.tensor_tensor(dst[:, h], t1[:, h, :].rearrange("c (m u e) -> c u m e", u=2, e=2), weight, ALU.mult)

        def quantise(turned, name):
            grouped = [sbuf([P, 4 * P], BF16, name + "_grouped%d" % h) for h in range(2)]
            codes = sbuf([P, S], U32, name + "_codes")
            scales = sbuf([P, S], U8, name + "_scales")
            words = turned[:].bitcast(F32)
            for h, (tag, copy) in enumerate(((6, nc.scalar.copy), (7, nc.vector.tensor_copy))):
                t2 = bank("t2", tag, [P, 2, P])
                for u in range(2):
                    nc.tensor.transpose(t2[:, u, :], words[:, (2 * h + u) * P : (2 * h + u + 1) * P], ident[:])
                dst = grouped[h][:].bitcast(F32).rearrange("p (c u) -> p c u", u=2)
                copy(dst, t2[:].rearrange("p u c -> p c u"))
            for h in range(2):
                cols = slice(h * P, (h + 1) * P)
                nc.vector.quantize_mx(
                    out=codes[:, cols].bitcast(FP8X4), scales=scales[:, cols], in_=grouped[h][:]
                )
            return codes, scales

        gather_scales("s_1a", [(x_sc, l_offs[:]), (x_sc, l_two[:]), (d_sc, part(l_k1, 0)), (d_sc, part(l_k2, 0))], plane_1a, nc.scalar)
        w_x1 = gather("w_x1", U32, [(x_w, l_offs[:]), (x_w, l_two[:])])
        w_1a = gather("w_1a", U32, [(d_w, part(l_k1, 0)), (d_w, part(l_k2, 0))])
        gather_scales("s_1b", [(d_sc, part(l_k1, 1)), (d_sc, part(l_k2, 1))], plane_1b, nc.sync, tag="s_1a")
        x_offs = (piece(w_x1, 0), piece(plane_1a, 0))
        x_two = (piece(w_x1, 1), piece(plane_1a, 1))


        def ratio_fetch(half, m1, m2):
            name = "r%d_" % half
            pa = sbuf([P, 2, W], F32, name + "pa")
            pb = sbuf([P, 2, W], F32, name + "pb")
            accs = [bank("acc", 2 * half + j, [P, S]) for j in range(2)]
            for j in range(2):
                product(accs[j], j, m1, x_offs, True, False)
            for j in range(2):
                product(accs[j], j, m2, x_two, False, True)
            for j in range(2):
                h = sbuf([P, S], F32, name + "h%d" % j)
                nc.scalar.activation(h[:], accs[j][:], ACT.Copy, scale=0.0625)
                fetch(pb[:, j, :], h, l_n2)
                fetch(pa[:, j, :], h, l_n1)
            size = sbuf([P, 2, W], F32, name + "size")
            seed = sbuf([P, 2, W], F32, name + "seed")
            nc.scalar.activation(size[:], pb[:], ACT.Abs)
            nc.scalar.activation(seed[:], size[:], ACT.Abs_reciprocal_sqrt, bias=0.5)
            return pa, pb, size, seed

        gain = sbuf([P, H], F32, "gain", tag="s_1a")
        nc.gpsimd.dma_start(gain[:], gs.rearrange("k o -> (k o)").partition_broadcast(P))
        z = [sbuf([P, S], F32, "z%d" % b) for b in range(4)]

        def ratio_factors(half, pa, pb, size, seed):
            name = "r%d_" % half
            rb = sbuf([P, 2, W], F32, name + "rb")
            nc.vector.tensor_tensor(rb[:], pa[:], pb[:], ALU.max)
            guess = sbuf([P, 2, W], F32, name + "guess")
            near_one = sbuf([P, 2, W], F32, name + "near_one")
            rough = sbuf([P, 2, W], F32, name + "rough")
            for j in range(2):
                nc.vector.tensor_tensor(guess[:, j, :], seed[:, j, :], seed[:, j, :], ALU.mult)
            for j in range(2):
                nc.vector.scalar_tensor_tensor(near_one[:, j, :], size[:, j, :], 0.5, guess[:, j, :], ALU.add, ALU.mult)
            for j in range(2):
                nc.vector.scalar_tensor_tensor(rough[:, j, :], pa[:, j, :], -1.0, guess[:, j, :], ALU.mult, ALU.mult)
            return rb, near_one, rough

        def ratio(half, near_one, rough, tag):
            ra = sbuf([P, 2, W], F32, "r%d_ra" % half, tag)
            nc.vector.scalar_tensor_tensor(ra[:], near_one[:], 2.0, rough[:], ALU.subtract, ALU.mult)
            return ra

        def put_pair(half, lst, values):
            for j in range(2):
                put(z[2 * half + j], lst, values[:, j, :])

        fetched = ratio_fetch(0, *[(piece(w_1a, n), piece(plane_1a, 2 + n)) for n in range(2)])
        w_1b = gather("w_1b", U32, [(d_w, part(l_k1, 1)), (d_w, part(l_k2, 1)), (d_w, part(l_k4, 0))], tag="w_1a")
        rb, near_one, rough = ratio_factors(0, *fetched)
        put_pair(0, l_n2, rb)
        gather_scales("s_4a", [(d_sc, part(l_k4, 0))], plane_4a, nc.sync, tag="r0_pb")
        gather_scales(
            "s_2a",
            [(d_sc, part(l_k5, 0)), (d_sc, part(l_k3, 0)), (x_sc, l_duo[:])],
            plane_2a, nc.sync, tag="r0_guess",
        )
        fetched = ratio_fetch(1, *[(piece(w_1b, n), piece(plane_1b, n)) for n in range(2)])
        put_pair(0, l_n1, ratio(0, near_one, rough, "r1_h1"))
        rb, near_one, rough = ratio_factors(1, *fetched)
        ra = ratio(1, near_one, rough, None)
        put_pair(1, l_n2, rb)
        put_pair(1, l_n1, ra)
        z_turned = sbuf([P, 4 * S], BF16, "z_turned", tag="r1_near_one")
        for b in range(2):
            turn_rows_weighted(z[b], z_turned, b, gain)
        gather_scales("s_hz", [(x_sc, l_hz[:])], plane_hz, nc.sync, tag="r1_guess")
        w_2a = gather("w_2a", U32, [(x_w, l_duo[:]), (x_w, l_hz[:]), (d_w, part(l_k5, 0))], tag="r1_rough")
        for b in range(2, 4):
            turn_rows_weighted(z[b], z_turned, b, gain)
        w_3a = gather("w_3a", U32, [(d_w, part(l_k3, 0))], tag="s_1a")
        z_codes, z_scales = quantise(z_turned, "z")
        gather_scales("s_2b", [(d_sc, part(l_k4, 1)), (d_sc, part(l_k5, 1)), (d_sc, part(l_k3, 1))], plane_2b, nc.sync, tag="z_grouped0")
        w_4b = gather("w_4b", U32, [(d_w, part(l_k4, 1))], tag="z_grouped1")

        x_duo = (piece(w_2a, 0), piece(plane_2a, 2))
        x_hz = (piece(w_2a, 1), plane_hz[:])
        z_mx = (z_codes[:], z_scales[:])
        out_turned = sbuf([P, 4 * S], BF16, "out_turned")

        def sort_fetch(half, m3, m4, m5):
            name = "s%d_" % half
            pa = sbuf([P, 2, W], F32, name + "pa")
            pb = sbuf([P, 2, W], F32, name + "pb")
            larger = sbuf([P, 2, W], F32, name + "larger")
            smaller = sbuf([P, 2, W], F32, name + "smaller")
            h2 = []
            accs = [bank("acc", 4 * half + j, [P, S]) for j in range(2)]
            for n, (weights, tokens) in enumerate(((m4, x_duo), (m5, x_hz), (m3, z_mx))):
                for j in range(2):
                    product(accs[j], j, weights, tokens, n == 0, n == 2)
            for j in range(2):
                acc = accs[j]
                h = sbuf([P, S], F32, name + "h%d" % j)
                if half == 0:
                    nc.scalar.activation(h[:], acc[:], ACT.Copy, scale=0.0625)
                else:
                    nc.vector.tensor_scalar(h[:], acc[:], 0.0625, None, ALU.mult)
                fetch(pa[:, j, :], h, l_n3)
                fetch(pb[:, j, :], h, l_n4)
                h2.append(h)
                nc.vector.tensor_tensor(larger[:, j, :], pa[:, j, :], pb[:, j, :], ALU.max)
            nc.vector.tensor_tensor(smaller[:], pa[:], pb[:], ALU.min)
            return h2, larger, smaller, accs

        def sort_put(half, larger, smaller):
            name = "s%d_" % half
            ub2 = [sbuf([P, S], F32, name + "u%d" % j) for j in range(2)]
            for j in range(2):
                put(ub2[j], l_n5, larger[:, j, :])
            for j in range(2):
                put(ub2[j], l_n6, smaller[:, j, :])
            return ub2

        def finish(half, h2, ub2, tag):
            y = sbuf([P, 2, S], F32, "y%d" % half, tag)
            for j in range(2):
                b = 2 * half + j
                nc.vector.tensor_tensor(y[:, j, :], ub2[j][:], h2[j][:], ALU.subtract)
                nc.sync.dma_start(out_0[b * P : (b + 1) * P, :], y[:, j, :])
            return y

        h2_0, larger, smaller, accs = sort_fetch(
            0, (w_3a[:], piece(plane_2a, 1)), (piece(w_1b, 2), plane_4a[:]), (piece(w_2a, 2), piece(plane_2a, 0))
        )
        w_53b = gather("w_53b", U32, [(d_w, part(l_k5, 1)), (d_w, part(l_k3, 1))], tag="s0_pa")
        ub2_0 = sort_put(0, larger, smaller)
        h2_1, larger, smaller, accs = sort_fetch(
            1, (piece(w_53b, 1), piece(plane_2b, 2)), (w_4b[:], piece(plane_2b, 0)), (piece(w_53b, 0), piece(plane_2b, 1))
        )
        y = finish(0, h2_0, ub2_0, "s0_pa")
        for j in range(2):
            turn_rows([y[:, j, :]], out_turned, j, nc.vector.tensor_copy)
        minus_h2 = sbuf([P, 2, S], F32, "minus_h2", tag="s1_pa")
        for j in range(2):
            nc.vector.tensor_scalar(minus_h2[:, j, :], accs[j][:], -0.0625, None, ALU.mult)
        ub2_1 = sort_put(1, larger, smaller)
        turn_rows([minus_h2[:, 0, :], ub2_1[0]], out_turned, 2, nc.scalar.copy)
        turn_last_rows([minus_h2[:, 1, :], ub2_1[1]], out_turned)
        finish(1, h2_1, ub2_1, None)

        y_codes, y_scales = quantise(out_turned, "y")
        for h in range(2):
            cols = slice(h * P, (h + 1) * P)
            nc.sync.dma_start(out_1[0].rearrange("p n t -> p (n t)").bitcast(I32)[:, cols], y_codes[:, cols].bitcast(I32))
        for i in range(4):
            queue = nc.scalar if i % 2 == 0 else nc.sync
            queue.dma_start(out_2[0][i:16:4, :].bitcast(I32), y_scales[i:P:32, :].bitcast(I32))
